import numpy as np
import ml_dtypes


def mxq(x, axis, fmt="e4m3"):
    dtype, down = {"e4m3": (ml_dtypes.float8_e4m3fn, 7), "e5m2": (ml_dtypes.float8_e5m2, 14)}[fmt]
    v = np.moveaxis(np.asarray(x, np.float32).astype(ml_dtypes.bfloat16).astype(np.float64), axis, -1)
    blocks = v.reshape(v.shape[:-1] + (-1, 32))
    amax = np.abs(blocks).max(-1, keepdims=True)
    byte = np.maximum(np.where(amax > 0, np.frexp(amax)[1] - 1 + 127, 0) - down, 1)
    scale = np.exp2(byte - 127.0)
    codes = (blocks / scale).astype(np.float32).astype(dtype).astype(np.float64)
    return np.moveaxis((codes * scale).reshape(v.shape), -1, axis)


WIDE = False


def mx_kscale(k):
    if not WIDE:
        return np.ones(k)
    levels = np.array([10, -10, 5, -5, 0])
    if k % 512:
        return np.exp2(np.random.permutation(np.resize(levels, k // 32))).repeat(32)
    a = np.empty((k // 512, 16))
    for p in range(k // 512):
        a[p, :8] = np.random.permutation(np.resize(levels, 8))
        for g in range(8):
            far = levels[np.abs(levels - a[p, g]) >= 10]
            a[p, g + 8] = far[np.random.randint(len(far))]
    return np.exp2(a.ravel()).repeat(32)


def f64(x):
    return np.asarray(x).astype(np.float64)


def striped(idx):
    return np.tile(idx.reshape(-1, 16).T, (8, 1)).astype(np.uint16)


def unstriped(offs):
    return offs[:16].T.reshape(-1).astype(np.int64)


def pack_weight(w):
    k, n = w.shape
    w = f64(np.asarray(w, np.float32).astype(ml_dtypes.bfloat16)).reshape(k // 32, 32, n)
    amax = np.abs(w).max(1)
    byte = np.clip(np.where(amax > 0, np.frexp(amax)[1] - 1 + 127 - 7, 1), 1, 254)
    scaled = (w * np.exp2(127.0 - byte)[:, None, :]).reshape(k, n).astype(np.float32)
    words = np.ascontiguousarray(scaled.reshape(k // 512, 128, 4, n).transpose(0, 1, 3, 2)).astype(ml_dtypes.float8_e4m3fn).view(np.uint8)
    return words, np.ascontiguousarray(byte.astype(np.uint8).reshape(k // 512, 16, n))


def unpack_weight(words, scales):
    g, p, n, _ = words.shape
    vals = np.ascontiguousarray(words).view(ml_dtypes.float8_e4m3fn).astype(np.float64) * np.repeat(np.exp2(scales.astype(np.float64) - 127.0), 8, axis=1)[..., None]
    return vals.transpose(0, 1, 3, 2).reshape(g * 512, n)

def planes(y):
    n, m = y.shape
    v = y.astype(np.float32).astype(ml_dtypes.bfloat16).astype(np.float64).reshape(n // 32, 32, m)
    top = np.abs(v).max(1)
    byte = np.clip(np.where(top > 0, np.frexp(top)[1] - 1 + 127 - 7, 1), 1, 254)
    codes = (v * np.exp2(127.0 - byte)[:, None, :]).reshape(n, m).astype(np.float32).astype(ml_dtypes.float8_e4m3fn).view(np.uint8)
    words = codes.reshape(n // 512, 128, 4, m).transpose(0, 1, 3, 2)
    return np.ascontiguousarray(words), np.ascontiguousarray(byte.astype(np.uint8).reshape(n // 512, 16, m))


K, T, S, H, W, C = 512, 2048, 512, 512, 256, 512


def setup_inputs():
    n = np.random.standard_normal
    s = mx_kscale(K)[:, None]
    packed_xT = pack_weight(n((K, T)) * s)
    packed_w1 = pack_weight(n((K, H)) / np.sqrt(K) / s)
    packed_w2 = pack_weight(n((K, H)) / np.sqrt(K) / s)
    return {
        "x_words": packed_xT[0],
        "x_scales": packed_xT[1],
        "w1_words": packed_w1[0],
        "w1_scales": packed_w1[1],
        "w2_words": packed_w2[0],
        "w2_scales": packed_w2[1],
        "gs": (np.random.uniform(0.5, 1.5, (K, 1)) / s).astype(np.float32),
        "offs": striped(np.random.permutation(T)[:S]),
        "two": striped(np.random.permutation(T)[:S]),
        "n1": striped(np.random.permutation(S)[:W]),
        "n2": striped(np.random.permutation(S)[:W]),
        "cand": striped(np.random.permutation(T)[:C]),
        "n3": striped(np.random.permutation(S)),
        "n4": striped(np.random.permutation(S)),
    }


def reference(x_words, x_scales, w1_words, w1_scales, w2_words, w2_scales, gs, offs, two, n1, n2, cand, n3, n4):
    x_cand = unpack_weight(x_words, x_scales)[:, unstriped(cand)]
    x_two = unpack_weight(x_words, x_scales)[:, unstriped(two)]
    d = unpack_weight(w2_words, w2_scales).T @ x_two
    xq = unpack_weight(x_words, x_scales)[:, unstriped(offs)]
    y = unpack_weight(w1_words, w1_scales).T @ xq
    ra = d[:, unstriped(n2)] - (0.5 * y[:, unstriped(n1)])
    ds = y.copy()
    ds[:, unstriped(n1)] = ra
    z = f64(gs) * ds
    s = 0.0625 * ((x_cand.T @ mxq(z, 0, "e4m3")))
    out_0 = s[:, unstriped(n3)] - s[:, unstriped(n4)]
    return (out_0,) + planes(out_0)

@@ -1,0 +1,174 @@
+from contextlib import ExitStack
+
+import concourse.mybir as mybir
+
+F32 = mybir.dt.float32
+BF16 = mybir.dt.bfloat16
+I32 = mybir.dt.int32
+U32 = mybir.dt.uint32
+U16 = mybir.dt.uint16
+U8 = mybir.dt.uint8
+FP8X4 = mybir.dt.float8_e4m3fn_x4
+COPY = mybir.ActivationFunctionType.Copy
+ADD = mybir.AluOpType.add
+SUB = mybir.AluOpType.subtract
+MULT = mybir.AluOpType.mult
+
+P = 128
+PACK = 4
+T = 2048
+S = 512
+W = 256
+HALF = 256
+FLOPS = 3 * 2 * 512 * 512 * 512
+
+
+def tile_picked_twcputbgap_none_po_kernel(
+    tc, x_words, x_scales, w1_words, w1_scales, w2_words, w2_scales, gs, offs, two, n1, n2, cand, n3, n4, out_0, out_1, out_2
+):
+    nc = tc.nc
+    with ExitStack() as ctx:
+        keep = ctx.enter_context(tc.tile_pool(name="keep", bufs=1))
+        psum = ctx.enter_context(tc.psum_pool(name="psum", bufs=1))
+
+        def load_list(name, dram):
+            tile = keep.tile(list(dram.shape), U16, name=name)
+            nc.sync.dma_start(tile[:], dram)
+            return tile
+
+        def load_scale_rows(engine, tile, first, dram):
+            for r in range(4):
+                engine.dma_start(tile[first + r : P : 32, :].bitcast(I32), dram[0][r:16:4, :].bitcast(I32))
+
+        def as_words(dram):
+            return dram[0].rearrange("p n t -> p (n t)").bitcast(I32)
+
+        xs = keep.tile([P, T], U8, name="xs", align_bytes=64)
+        nc.vector.memset(xs[:].bitcast(I32), 0)
+        ws_raw = keep.tile([P, S], U8, name="ws_raw", align_bytes=64)
+        nc.vector.memset(ws_raw[:].bitcast(I32), 0)
+
+        offs_t = load_list("offs_t", offs)
+        load_scale_rows(nc.scalar, xs, 0, x_scales)
+        two_t = load_list("two_t", two)
+        xw = keep.tile([P, T], I32, name="xw", align_bytes=64)
+        nc.sync.dma_start(xw[:], as_words(x_words))
+        w_raw = []
+        for i, dram in enumerate((w1_words, w2_words)):
+            tile = keep.tile([P, S], I32, name="w_raw%d" % i, align_bytes=64)
+            nc.sync.dma_start(tile[:], as_words(dram))
+            w_raw.append(tile)
+        load_scale_rows(nc.scalar, ws_raw, 0, w1_scales)
+        load_scale_rows(nc.scalar, ws_raw, 4, w2_scales)
+        cand_t = load_list("cand_t", cand)
+        n1_t = load_list("n1_t", n1)
+        n2_t = load_list("n2_t", n2)
+        gs_t = keep.tile([P, PACK], F32, name="gs_t")
+        nc.sync.dma_start(gs_t[:], gs.rearrange("(p t) o -> p (t o)", t=PACK))
+        n3_t = load_list("n3_t", n3)
+        n4_t = load_list("n4_t", n4)
+
+        def dealt(ap):
+            return ap.rearrange("p (t m) -> p m t", t=PACK)
+
+        def plain(ap):
+            return ap.rearrange("p (m t) -> p m t", t=PACK)
+
+        def gather_scales(name, lst):
+            tile = keep.tile([P, S], U8, name=name, align_bytes=64)
+            nc.vector.tensor_copy(tile[:], xs[:].indirect(lst[:]))
+            return tile
+
+        def gather_words(name, lst, view):
+            tile = keep.tile([P, S], U32, name=name, align_bytes=64)
+            nc.vector.tensor_copy(view(tile[:]), xw[:].bitcast(U32).indirect(lst[:]))
+            return tile
+
+        def deal(name, dtype, src):
+            tile = keep.tile([P, S], dtype, name=name, align_bytes=64)
+            nc.vector.tensor_copy(dealt(tile[:]), plain(src[:]))
+            return tile
+
+        xo_s = gather_scales("xo_s", offs_t)
+        xt_s = gather_scales("xt_s", two_t)
+        xo_w = gather_words("xo_w", offs_t, lambda ap: ap)
+        w1_d = deal("w1_d", I32, w_raw[0])
+        ws = deal("ws", U8, ws_raw)
+        xt_w = gather_words("xt_w", two_t, lambda ap: ap)
+        w2_d = deal("w2_d", I32, w_raw[1])
+        xc_s_raw = gather_scales("xc_s_raw", cand_t)
+        xc_w = gather_words("xc_w", cand_t, dealt)
+        xc_s = deal("xc_s", U8, xc_s_raw)
+
+        def product(t, bank, lhs_w, lhs_s, first, rhs_w, rhs_s):
+            cols = slice(P * t, P * (t + 1))
+            acc = psum.tile([P, S], F32, name="acc", tag="bank%d" % bank)
+            nc.tensor.matmul_mx(
+                out=acc[:],
+                lhsT=lhs_w[:, cols].bitcast(FP8X4),
+                lhsT_scale=lhs_s[first:P, cols],
+                rhs=rhs_w[:].bitcast(FP8X4),
+                rhs_scale=rhs_s[:],
+                start=True,
+                stop=True,
+            )
+            return acc
+
+        y_acc = [product(t, t, w1_d, ws, 0, xo_w, xo_s) for t in range(PACK)]
+        d_acc = [product(t, PACK + t, w2_d, ws, 4, xt_w, xt_s) for t in range(PACK)]
+
+        ds = []
+        y_half = []
+        for t in range(PACK):
+            tile = keep.tile([P, S], F32, name="ds%d" % t)
+            nc.scalar.activation(tile[:], y_acc[t][:], COPY)
+            ds.append(tile)
+            g = keep.tile([P, W], F32, name="y_half%d" % t)
+            nc.scalar.activation(g[:], tile[:].indirect(n1_t[:]), COPY, scale=-0.5)
+            y_half.append(g)
+
+        z_planes = keep.tile([P, PACK, S], BF16, name="z_planes", align_bytes=64)
+        for t in range(PACK):
+            d_sb = keep.tile([P, S], F32, name="d_sb%d" % t)
+            nc.scalar.activation(d_sb[:], d_acc[t][:], COPY)
+            g = keep.tile([P, W], F32, name="d_pick%d" % t)
+            nc.scalar.activation(g[:], d_sb[:].indirect(n2_t[:]), COPY)
+            nc.vector.tensor_tensor(ds[t][:].indirect(n1_t[:]), g[:], y_half[t][:], ADD)
+            nc.vector.tensor_scalar(z_planes[:, t, :], ds[t][:], gs_t[:, t : t + 1], None, MULT)
+
+        z_in = keep.tile([P, S, PACK], BF16, name="z_in", align_bytes=64)
+        nc.vector.tensor_copy(z_in[:], z_planes[:].rearrange("p t j -> p j t"))
+        z_w = keep.tile([P, S], U32, name="z_w", align_bytes=64)
+        z_s = keep.tile([P, S], U8, name="z_s", align_bytes=64)
+        nc.vector.quantize_mx(out=z_w[:].bitcast(FP8X4), scales=z_s[:], in_=z_in[:].rearrange("p j t -> p (j t)"))
+
+        neg_s = []
+        for t in range(PACK):
+            acc = product(t, t, xc_w, xc_s, 0, z_w, z_s)
+            tile = keep.tile([P, S], F32, name="neg_s%d" % t)
+            if t % 2 == 0:
+                nc.scalar.activation(tile[:], acc[:], COPY, scale=-0.0625)
+            else:
+                nc.vector.tensor_scalar(tile[:], acc[:], -0.0625, None, MULT)
+            neg_s.append(tile)
+
+        out_rows = out_0.rearrange("(p t) j -> p t j", t=PACK)
+        o_w = keep.tile([P, S], I32, name="o_w", align_bytes=64)
+        o_s = keep.tile([P, S], U8, name="o_s", align_bytes=64)
+        for h in range(2):
+            cols = slice(h * HALF, (h + 1) * HALF)
+            entries = slice(h * HALF // 16, (h + 1) * HALF // 16)
+            o = keep.tile([P, PACK, HALF], F32, name="o%d" % h)
+            for t in range(PACK):
+                g = keep.tile([P, HALF], F32, name="g3_%d_%d" % (h, t))
+                nc.scalar.activation(g[:], neg_s[t][:].indirect(n3_t[:, entries]), COPY)
+                nc.vector.tensor_tensor(o[:, t, :], neg_s[t][:].indirect(n4_t[:, entries]), g[:], SUB)
+                if t % 2 == 1:
+                    nc.sync.dma_start(out_rows[:, t - 1 : t + 1, cols], o[:, t - 1 : t + 1, :])
+            o_in = keep.tile([P, HALF, PACK], BF16, name="o_in%d" % h, align_bytes=64)
+            nc.vector.tensor_copy(o_in[:], o[:].rearrange("p t j -> p j t"))
+            nc.vector.quantize_mx(out=o_w[:, cols].bitcast(FP8X4), scales=o_s[:, cols], in_=o_in[:].rearrange("p j t -> p (j t)"))
+            nc.sync.dma_start(as_words(out_1)[:, cols], o_w[:, cols])
+        for r in range(4):
+            engine = nc.sync if r % 2 == 0 else nc.scalar
+            engine.dma_start(out_2[0][r:16:4, :].bitcast(I32), o_s[r:P:32, :].bitcast(I32))

@@ -45,23 +45,26 @@ def tile_picked_twcputbgap_none_po_kernel(
 
         xs = keep.tile([P, T], U8, name="xs", align_bytes=64)
         nc.vector.memset(xs[:].bitcast(I32), 0)
-        ws_raw = keep.tile([P, S], U8, name="ws_raw", align_bytes=64)
-        nc.vector.memset(ws_raw[:].bitcast(I32), 0)
+        w1s_raw = keep.tile([P, S], U8, name="w1s_raw", tag="reuse_a", align_bytes=64)
+        nc.gpsimd.memset(w1s_raw[:].bitcast(I32), 0)
+        w2s_raw = keep.tile([P, S], U8, name="w2s_raw", tag="w2s_raw", align_bytes=64)
+        nc.gpsimd.memset(w2s_raw[:].bitcast(I32), 0)
 
-        offs_t = load_list("offs_t", offs)
-        load_scale_rows(nc.scalar, xs, 0, x_scales)
-        two_t = load_list("two_t", two)
-        xw = keep.tile([P, T], I32, name="xw", align_bytes=64)
-        nc.sync.dma_start(xw[:], as_words(x_words))
-        w_raw = []
-        for i, dram in enumerate((w1_words, w2_words)):
-            tile = keep.tile([P, S], I32, name="w_raw%d" % i, align_bytes=64)
+        def load_words(name, tag, dram, width):
+            tile = keep.tile([P, width], I32, name=name, tag=tag, align_bytes=64)
             nc.sync.dma_start(tile[:], as_words(dram))
-            w_raw.append(tile)
-        load_scale_rows(nc.scalar, ws_raw, 0, w1_scales)
-        load_scale_rows(nc.scalar, ws_raw, 4, w2_scales)
-        cand_t = load_list("cand_t", cand)
+            return tile
+
+        load_scale_rows(nc.sync, xs, 0, x_scales)
+        offs_t = load_list("offs_t", offs)
+        w1_raw = load_words("w1_raw", "w1_raw", w1_words, S)
+        w2_raw = load_words("w2_raw", "w2_raw", w2_words, S)
+        xw = load_words("xw", "xw", x_words, T)
+        two_t = load_list("two_t", two)
+        load_scale_rows(nc.sync, w1s_raw, 0, w1_scales)
         n1_t = load_list("n1_t", n1)
+        load_scale_rows(nc.sync, w2s_raw, 0, w2_scales)
+        cand_t = load_list("cand_t", cand)
         n2_t = load_list("n2_t", n2)
         gs_t = keep.tile([P, PACK], F32, name="gs_t")
         nc.sync.dma_start(gs_t[:], gs.rearrange("(p t) o -> p (t o)", t=PACK))
@@ -74,13 +77,13 @@ def tile_picked_twcputbgap_none_po_kernel(
         def plain(ap):
             return ap.rearrange("p (m t) -> p m t", t=PACK)
 
-        def gather_scales(name, lst):
-            tile = keep.tile([P, S], U8, name=name, align_bytes=64)
+        def gather_scales(name, tag, lst):
+            tile = keep.tile([P, S], U8, name=name, tag=tag, align_bytes=64)
             nc.vector.tensor_copy(tile[:], xs[:].indirect(lst[:]))
             return tile
 
-        def gather_words(name, lst, view):
-            tile = keep.tile([P, S], U32, name=name, align_bytes=64)
+        def gather_words(name, tag, lst, view):
+            tile = keep.tile([P, S], U32, name=name, tag=tag, align_bytes=64)
             nc.vector.tensor_copy(view(tile[:]), xw[:].bitcast(U32).indirect(lst[:]))
             return tile
 
@@ -89,15 +92,16 @@ def tile_picked_twcputbgap_none_po_kernel(
             nc.vector.tensor_copy(dealt(tile[:]), plain(src[:]))
             return tile
 
-        xo_s = gather_scales("xo_s", offs_t)
-        xt_s = gather_scales("xt_s", two_t)
-        xo_w = gather_words("xo_w", offs_t, lambda ap: ap)
-        w1_d = deal("w1_d", I32, w_raw[0])
-        ws = deal("ws", U8, ws_raw)
-        xt_w = gather_words("xt_w", two_t, lambda ap: ap)
-        w2_d = deal("w2_d", I32, w_raw[1])
-        xc_s_raw = gather_scales("xc_s_raw", cand_t)
-        xc_w = gather_words("xc_w", cand_t, dealt)
+        xo_s = gather_scales("xo_s", "xo_s", offs_t)
+        xo_w = gather_words("xo_w", "xo_w", offs_t, lambda ap: ap)
+        w1_d = deal("w1_d", I32, w1_raw)
+        w1_s = deal("w1_s", U8, w1s_raw)
+        xt_s = gather_scales("xt_s", "xt_s", two_t)
+        xt_w = gather_words("xt_w", "reuse_a", two_t, lambda ap: ap)
+        w2_s = deal("w2_s", U8, w2s_raw)
+        w2_d = deal("w2_d", I32, w2_raw)
+        xc_s_raw = gather_scales("xc_s_raw", "xc_s_raw", cand_t)
+        xc_w = gather_words("xc_w", "xc_w", cand_t, dealt)
         xc_s = deal("xc_s", U8, xc_s_raw)
 
         def product(t, bank, lhs_w, lhs_s, first, rhs_w, rhs_s):
@@ -114,27 +118,21 @@ def tile_picked_twcputbgap_none_po_kernel(
             )
             return acc
 
-        y_acc = [product(t, t, w1_d, ws, 0, xo_w, xo_s) for t in range(PACK)]
-        d_acc = [product(t, PACK + t, w2_d, ws, 4, xt_w, xt_s) for t in range(PACK)]
-
-        ds = []
-        y_half = []
-        for t in range(PACK):
-            tile = keep.tile([P, S], F32, name="ds%d" % t)
-            nc.scalar.activation(tile[:], y_acc[t][:], COPY)
-            ds.append(tile)
-            g = keep.tile([P, W], F32, name="y_half%d" % t)
-            nc.scalar.activation(g[:], tile[:].indirect(n1_t[:]), COPY, scale=-0.5)
-            y_half.append(g)
+        y_acc = [product(t, t, w1_d, w1_s, 0, xo_w, xo_s) for t in range(PACK)]
+        d_acc = [product(t, PACK + t, w2_d, w2_s, 0, xt_w, xt_s) for t in range(PACK)]
 
         z_planes = keep.tile([P, PACK, S], BF16, name="z_planes", align_bytes=64)
         for t in range(PACK):
+            ds = keep.tile([P, S], F32, name="ds%d" % t)
+            nc.scalar.activation(ds[:], y_acc[t][:], COPY)
+            y_half = keep.tile([P, W], F32, name="y_half%d" % t)
+            nc.scalar.activation(y_half[:], ds[:].indirect(n1_t[:]), COPY, scale=-0.5)
             d_sb = keep.tile([P, S], F32, name="d_sb%d" % t)
             nc.scalar.activation(d_sb[:], d_acc[t][:], COPY)
-            g = keep.tile([P, W], F32, name="d_pick%d" % t)
-            nc.scalar.activation(g[:], d_sb[:].indirect(n2_t[:]), COPY)
-            nc.vector.tensor_tensor(ds[t][:].indirect(n1_t[:]), g[:], y_half[t][:], ADD)
-            nc.vector.tensor_scalar(z_planes[:, t, :], ds[t][:], gs_t[:, t : t + 1], None, MULT)
+            d_pick = keep.tile([P, W], F32, name="d_pick%d" % t)
+            nc.scalar.activation(d_pick[:], d_sb[:].indirect(n2_t[:]), COPY)
+            nc.vector.tensor_tensor(ds[:].indirect(n1_t[:]), d_pick[:], y_half[:], ADD)
+            nc.vector.tensor_scalar(z_planes[:, t, :], ds[:], gs_t[:, t : t + 1], None, MULT)
 
         z_in = keep.tile([P, S, PACK], BF16, name="z_in", align_bytes=64)
         nc.vector.tensor_copy(z_in[:], z_planes[:].rearrange("p t j -> p j t"))
@@ -146,7 +144,7 @@ def tile_picked_twcputbgap_none_po_kernel(
         for t in range(PACK):
             acc = product(t, t, xc_w, xc_s, 0, z_w, z_s)
             tile = keep.tile([P, S], F32, name="neg_s%d" % t)
-            if t % 2 == 0:
+            if t != 1:
                 nc.scalar.activation(tile[:], acc[:], COPY, scale=-0.0625)
             else:
                 nc.vector.tensor_scalar(tile[:], acc[:], -0.0625, None, MULT)
@@ -155,6 +153,7 @@ def tile_picked_twcputbgap_none_po_kernel(
         out_rows = out_0.rearrange("(p t) j -> p t j", t=PACK)
         o_w = keep.tile([P, S], I32, name="o_w", align_bytes=64)
         o_s = keep.tile([P, S], U8, name="o_s", align_bytes=64)
+        halves = []
         for h in range(2):
             cols = slice(h * HALF, (h + 1) * HALF)
             entries = slice(h * HALF // 16, (h + 1) * HALF // 16)
@@ -165,8 +164,14 @@ def tile_picked_twcputbgap_none_po_kernel(
                 nc.vector.tensor_tensor(o[:, t, :], neg_s[t][:].indirect(n4_t[:, entries]), g[:], SUB)
                 if t % 2 == 1:
                     nc.sync.dma_start(out_rows[:, t - 1 : t + 1, cols], o[:, t - 1 : t + 1, :])
+            halves.append(o)
+        for h in range(2):
+            cols = slice(h * HALF, (h + 1) * HALF)
             o_in = keep.tile([P, HALF, PACK], BF16, name="o_in%d" % h, align_bytes=64)
-            nc.vector.tensor_copy(o_in[:], o[:].rearrange("p t j -> p j t"))
+            if h == 0:
+                nc.scalar.copy(o_in[:], halves[h][:].rearrange("p t j -> p j t"))
+            else:
+                nc.vector.tensor_copy(o_in[:], halves[h][:].rearrange("p t j -> p j t"))
             nc.vector.quantize_mx(out=o_w[:, cols].bitcast(FP8X4), scales=o_s[:, cols], in_=o_in[:].rearrange("p j t -> p (j t)"))
             nc.sync.dma_start(as_words(out_1)[:, cols], o_w[:, cols])
         for r in range(4):

@@ -36,34 +36,33 @@ def tile_picked_twcputbgap_none_po_kernel(
             nc.sync.dma_start(tile[:], dram)
             return tile
 
-        def load_scale_rows(engine, tile, first, dram):
-            for r in range(4):
-                engine.dma_start(tile[first + r : P : 32, :].bitcast(I32), dram[0][r:16:4, :].bitcast(I32))
+        def load_scale_rows(engine, tile, first, dram, r):
+            engine.dma_start(tile[first + r : P : 32, :].bitcast(I32), dram[0][r:16:4, :].bitcast(I32))
 
         def as_words(dram):
             return dram[0].rearrange("p n t -> p (n t)").bitcast(I32)
 
         xs = keep.tile([P, T], U8, name="xs", align_bytes=64)
-        nc.vector.memset(xs[:].bitcast(I32), 0)
-        w1s_raw = keep.tile([P, S], U8, name="w1s_raw", tag="reuse_a", align_bytes=64)
-        nc.gpsimd.memset(w1s_raw[:].bitcast(I32), 0)
-        w2s_raw = keep.tile([P, S], U8, name="w2s_raw", tag="w2s_raw", align_bytes=64)
-        nc.gpsimd.memset(w2s_raw[:].bitcast(I32), 0)
+        ws_raw = keep.tile([P, S], U8, name="ws_raw", tag="reuse_a", align_bytes=64)
+        nc.gpsimd.memset(ws_raw[:].bitcast(I32), 0)
 
         def load_words(name, tag, dram, width):
             tile = keep.tile([P, width], I32, name=name, tag=tag, align_bytes=64)
             nc.sync.dma_start(tile[:], as_words(dram))
             return tile
 
-        load_scale_rows(nc.sync, xs, 0, x_scales)
+        for q in range(4):
+            rows = x_scales[0][4 * q : 4 * q + 4, :].bitcast(I32).rearrange("r n -> (r n)")
+            nc.sync.dma_start(xs[32 * q : 32 * q + 32, :].bitcast(I32), rows.partition_broadcast(8))
         offs_t = load_list("offs_t", offs)
-        w1_raw = load_words("w1_raw", "w1_raw", w1_words, S)
-        w2_raw = load_words("w2_raw", "w2_raw", w2_words, S)
-        xw = load_words("xw", "xw", x_words, T)
         two_t = load_list("two_t", two)
-        load_scale_rows(nc.sync, w1s_raw, 0, w1_scales)
+        w1_raw = load_words("w1_raw", "w1_raw", w1_words, S)
+        xw = load_words("xw", "xw", x_words, T)
+        for r in range(4):
+            load_scale_rows(nc.sync, ws_raw, 0, w1_scales, r)
+            load_scale_rows(nc.sync if r < 3 else nc.gpsimd, ws_raw, 4, w2_scales, r)
+        w2_raw = load_words("w2_raw", "w2_raw", w2_words, S)
         n1_t = load_list("n1_t", n1)
-        load_scale_rows(nc.sync, w2s_raw, 0, w2_scales)
         cand_t = load_list("cand_t", cand)
         n2_t = load_list("n2_t", n2)
         gs_t = keep.tile([P, PACK], F32, name="gs_t")
@@ -74,8 +73,8 @@ def tile_picked_twcputbgap_none_po_kernel(
         def dealt(ap):
             return ap.rearrange("p (t m) -> p m t", t=PACK)
 
-        def plain(ap):
-            return ap.rearrange("p (m t) -> p m t", t=PACK)
+        def weave(copy, out, planes):
+            copy(out.rearrange("p (c i) t -> p c t i", i=4), planes.rearrange("p t (c i) -> p c t i", i=4))
 
         def gather_scales(name, tag, lst):
             tile = keep.tile([P, S], U8, name=name, tag=tag, align_bytes=64)
@@ -87,22 +86,24 @@ def tile_picked_twcputbgap_none_po_kernel(
             nc.vector.tensor_copy(view(tile[:]), xw[:].bitcast(U32).indirect(lst[:]))
             return tile
 
-        def deal(name, dtype, src):
+        def deal(name, dtype, src, line):
             tile = keep.tile([P, S], dtype, name=name, align_bytes=64)
-            nc.vector.tensor_copy(dealt(tile[:]), plain(src[:]))
+            nc.vector.tensor_copy(
+                tile[:].rearrange("p (t c i) -> p c t i", t=PACK, i=line),
+                src[:].rearrange("p (c i t) -> p c t i", t=PACK, i=line),
+            )
             return tile
 
         xo_s = gather_scales("xo_s", "xo_s", offs_t)
         xo_w = gather_words("xo_w", "xo_w", offs_t, lambda ap: ap)
-        w1_d = deal("w1_d", I32, w1_raw)
-        w1_s = deal("w1_s", U8, w1s_raw)
+        w1_d = deal("w1_d", I32, w1_raw, 4)
+        ws = deal("ws", U8, ws_raw, 16)
         xt_s = gather_scales("xt_s", "xt_s", two_t)
         xt_w = gather_words("xt_w", "reuse_a", two_t, lambda ap: ap)
-        w2_s = deal("w2_s", U8, w2s_raw)
-        w2_d = deal("w2_d", I32, w2_raw)
+        w2_d = deal("w2_d", I32, w2_raw, 4)
         xc_s_raw = gather_scales("xc_s_raw", "xc_s_raw", cand_t)
         xc_w = gather_words("xc_w", "xc_w", cand_t, dealt)
-        xc_s = deal("xc_s", U8, xc_s_raw)
+        xc_s = deal("xc_s", U8, xc_s_raw, 16)
 
         def product(t, bank, lhs_w, lhs_s, first, rhs_w, rhs_s):
             cols = slice(P * t, P * (t + 1))
@@ -118,36 +119,73 @@ def tile_picked_twcputbgap_none_po_kernel(
             )
             return acc
 
-        y_acc = [product(t, t, w1_d, w1_s, 0, xo_w, xo_s) for t in range(PACK)]
-        d_acc = [product(t, PACK + t, w2_d, w2_s, 0, xt_w, xt_s) for t in range(PACK)]
+        y_acc = [product(t, t, w1_d, ws, 0, xo_w, xo_s) for t in range(PACK)]
+        d_acc = [product(t, PACK + t, w2_d, ws, 4, xt_w, xt_s) for t in range(PACK)]
 
         z_planes = keep.tile([P, PACK, S], BF16, name="z_planes", align_bytes=64)
-        for t in range(PACK):
-            ds = keep.tile([P, S], F32, name="ds%d" % t)
-            nc.scalar.activation(ds[:], y_acc[t][:], COPY)
-            y_half = keep.tile([P, W], F32, name="y_half%d" % t)
-            nc.scalar.activation(y_half[:], ds[:].indirect(n1_t[:]), COPY, scale=-0.5)
-            d_sb = keep.tile([P, S], F32, name="d_sb%d" % t)
-            nc.scalar.activation(d_sb[:], d_acc[t][:], COPY)
-            d_pick = keep.tile([P, W], F32, name="d_pick%d" % t)
-            nc.scalar.activation(d_pick[:], d_sb[:].indirect(n2_t[:]), COPY)
-            nc.vector.tensor_tensor(ds[:].indirect(n1_t[:]), d_pick[:], y_half[:], ADD)
+        def round_plane(t, ds):
             nc.vector.tensor_scalar(z_planes[:, t, :], ds[:], gs_t[:, t : t + 1], None, MULT)
 
-        z_in = keep.tile([P, S, PACK], BF16, name="z_in", align_bytes=64)
-        nc.vector.tensor_copy(z_in[:], z_planes[:].rearrange("p t j -> p j t"))
+        ds_all = []
+        for t in range(PACK):
+            on_scalar = t == 2
+            ds = keep.tile([P, S], F32, name="ds%d" % t)
+            nc.scalar.activation(ds[:], y_acc[t][:], COPY)
+            d_sb = keep.tile([P, S], F32, name="d_sb%d" % t)
+            nc.scalar.activation(d_sb[:], d_acc[t][:], COPY, scale=2.0 if on_scalar else 1.0)
+            y_half = keep.tile([P, W], F32, name="y_half%d" % t)
+            d_pick = keep.tile([P, W], F32, name="d_pick%d" % t)
+            if on_scalar:
+                nc.scalar.activation(d_pick[:], d_sb[:].indirect(n2_t[:]), COPY)
+                nc.vector.tensor_tensor(y_half[:], ds[:].indirect(n1_t[:]), d_pick[:], SUB)
+                late = y_half
+            else:
+                nc.scalar.activation(y_half[:], ds[:].indirect(n1_t[:]), COPY, scale=-0.5)
+                nc.scalar.activation(d_pick[:], d_sb[:].indirect(n2_t[:]), COPY)
+                nc.vector.tensor_tensor(ds[:].indirect(n1_t[:]), d_pick[:], y_half[:], ADD)
+            ds_all.append(ds)
+            if t in (1, 2):
+                round_plane(t - 1, ds_all[t - 1])
+        nc.scalar.activation(ds_all[2][:].indirect(n1_t[:]), late[:], COPY, scale=-0.5)
+        round_plane(3, ds_all[3])
+        nc.scalar.activation(z_planes[:, 2, :], ds_all[2][:], COPY, scale=gs_t[:, 2:3])
+
         z_w = keep.tile([P, S], U32, name="z_w", align_bytes=64)
         z_s = keep.tile([P, S], U8, name="z_s", align_bytes=64)
-        nc.vector.quantize_mx(out=z_w[:].bitcast(FP8X4), scales=z_s[:], in_=z_in[:].rearrange("p j t -> p (j t)"))
+        z_in = keep.tile([P, S, PACK], BF16, name="z_in", align_bytes=64)
+        weave(nc.vector.tensor_copy, z_in[:, 0:256, :], z_planes[:, :, 0:256])
+        weave(nc.vector.tensor_copy, z_in[:, 256:384, :], z_planes[:, :, 256:384])
+        weave(nc.scalar.copy, z_in[:, 384:512, :], z_planes[:, :, 384:512])
+        s_acc = [psum.tile([P, S], F32, name="s_acc%d" % t, tag="bank%d" % t) for t in range(PACK)]
+        for h in range(2):
+            cols = slice(h * HALF, (h + 1) * HALF)
+            nc.vector.quantize_mx(out=z_w[:, cols].bitcast(FP8X4), scales=z_s[:, cols], in_=z_in[:, cols, :].rearrange("p j t -> p (j t)"))
+
+        def score(t, cols):
+            rows = slice(P * t, P * (t + 1))
+            nc.tensor.matmul_mx(
+                out=s_acc[t][:, cols],
+                lhsT=xc_w[:, rows].bitcast(FP8X4),
+                lhsT_scale=xc_s[:, rows],
+                rhs=z_w[:, cols].bitcast(FP8X4),
+                rhs_scale=z_s[:, cols],
+                start=True,
+                stop=True,
+            )
+
+        for h in range(2):
+            for t in range(2):
+                score(t, slice(h * HALF, (h + 1) * HALF))
+        for t in range(2, PACK):
+            score(t, slice(0, S))
 
         neg_s = []
         for t in range(PACK):
-            acc = product(t, t, xc_w, xc_s, 0, z_w, z_s)
             tile = keep.tile([P, S], F32, name="neg_s%d" % t)
-            if t != 1:
-                nc.scalar.activation(tile[:], acc[:], COPY, scale=-0.0625)
+            if t % 2 == 0:
+                nc.scalar.activation(tile[:], s_acc[t][:], COPY, scale=-0.0625)
             else:
-                nc.vector.tensor_scalar(tile[:], acc[:], -0.0625, None, MULT)
+                nc.vector.tensor_scalar(tile[:], s_acc[t][:], -0.0625, None, MULT)
             neg_s.append(tile)
 
         out_rows = out_0.rearrange("(p t) j -> p t j", t=PACK)
@@ -161,7 +199,12 @@ def tile_picked_twcputbgap_none_po_kernel(
             for t in range(PACK):
                 g = keep.tile([P, HALF], F32, name="g3_%d_%d" % (h, t))
                 nc.scalar.activation(g[:], neg_s[t][:].indirect(n3_t[:, entries]), COPY)
-                nc.vector.tensor_tensor(o[:, t, :], neg_s[t][:].indirect(n4_t[:, entries]), g[:], SUB)
+                if t == PACK - 1:
+                    g4 = keep.tile([P, HALF], F32, name="g4_%d" % h)
+                    nc.scalar.activation(g4[:], neg_s[t][:].indirect(n4_t[:, entries]), COPY)
+                    nc.vector.tensor_tensor(o[:, t, :], g4[:], g[:], SUB)
+                else:
+                    nc.vector.tensor_tensor(o[:, t, :], neg_s[t][:].indirect(n4_t[:, entries]), g[:], SUB)
                 if t % 2 == 1:
                     nc.sync.dma_start(out_rows[:, t - 1 : t + 1, cols], o[:, t - 1 : t + 1, :])
             halves.append(o)
@@ -169,9 +212,9 @@ def tile_picked_twcputbgap_none_po_kernel(
             cols = slice(h * HALF, (h + 1) * HALF)
             o_in = keep.tile([P, HALF, PACK], BF16, name="o_in%d" % h, align_bytes=64)
             if h == 0:
-                nc.scalar.copy(o_in[:], halves[h][:].rearrange("p t j -> p j t"))
+                weave(nc.scalar.copy, o_in[:], halves[h][:])
             else:
-                nc.vector.tensor_copy(o_in[:], halves[h][:].rearrange("p t j -> p j t"))
+                weave(nc.vector.tensor_copy, o_in[:], halves[h][:])
             nc.vector.quantize_mx(out=o_w[:, cols].bitcast(FP8X4), scales=o_s[:, cols], in_=o_in[:].rearrange("p j t -> p (j t)"))
             nc.sync.dma_start(as_words(out_1)[:, cols], o_w[:, cols])
         for r in range(4):

@@ -16,10 +16,19 @@ MULT = mybir.AluOpType.mult
 
 P = 128
 PACK = 4
+QUADRANT = 32
+SCALE_ROWS = 16
 T = 2048
 S = 512
 W = 256
-HALF = 256
+HALF = S // 2
+LIST_COLS = HALF // 16
+W2_ROWS = 4
+WORDS_A_LINE = 4
+BYTES_A_LINE = 16
+WEAVE_RUN = 4
+Z_SPLIT = 384
+NEG_SIXTEENTH = -0.0625
 FLOPS = 3 * 2 * 512 * 512 * 512
 
 
@@ -31,37 +40,37 @@ def tile_picked_twcputbgap_none_po_kernel(
         keep = ctx.enter_context(tc.tile_pool(name="keep", bufs=1))
         psum = ctx.enter_context(tc.psum_pool(name="psum", bufs=1))
 
+        def as_words(dram):
+            return dram[0].rearrange("p n t -> p (n t)").bitcast(I32)
+
         def load_list(name, dram):
             tile = keep.tile(list(dram.shape), U16, name=name)
             nc.sync.dma_start(tile[:], dram)
             return tile
 
-        def load_scale_rows(engine, tile, first, dram, r):
-            engine.dma_start(tile[first + r : P : 32, :].bitcast(I32), dram[0][r:16:4, :].bitcast(I32))
-
-        def as_words(dram):
-            return dram[0].rearrange("p n t -> p (n t)").bitcast(I32)
-
-        xs = keep.tile([P, T], U8, name="xs", align_bytes=64)
-        ws_raw = keep.tile([P, S], U8, name="ws_raw", tag="reuse_a", align_bytes=64)
-        nc.gpsimd.memset(ws_raw[:].bitcast(I32), 0)
-
-        def load_words(name, tag, dram, width):
-            tile = keep.tile([P, width], I32, name=name, tag=tag, align_bytes=64)
+        def load_words(name, dram, width):
+            tile = keep.tile([P, width], I32, name=name, align_bytes=64)
             nc.sync.dma_start(tile[:], as_words(dram))
             return tile
 
-        for q in range(4):
-            rows = x_scales[0][4 * q : 4 * q + 4, :].bitcast(I32).rearrange("r n -> (r n)")
-            nc.sync.dma_start(xs[32 * q : 32 * q + 32, :].bitcast(I32), rows.partition_broadcast(8))
+        def load_scale_rows(engine, tile, first, dram, r):
+            engine.dma_start(tile[first + r : P : QUADRANT, :].bitcast(I32), dram[0][r:SCALE_ROWS:PACK, :].bitcast(I32))
+
+        xs = keep.tile([P, T], U8, name="xs", align_bytes=64)
+        ws_raw = keep.tile([P, S], U8, name="ws_raw", tag="ws_raw_then_xt_w", align_bytes=64)
+        nc.gpsimd.memset(ws_raw[:].bitcast(I32), 0)
+
+        for q in range(P // QUADRANT):
+            rows = x_scales[0][PACK * q : PACK * (q + 1), :].bitcast(I32).rearrange("r n -> (r n)")
+            nc.sync.dma_start(xs[QUADRANT * q : QUADRANT * (q + 1), :].bitcast(I32), rows.partition_broadcast(QUADRANT // PACK))
         offs_t = load_list("offs_t", offs)
         two_t = load_list("two_t", two)
-        w1_raw = load_words("w1_raw", "w1_raw", w1_words, S)
-        xw = load_words("xw", "xw", x_words, T)
-        for r in range(4):
+        w1_raw = load_words("w1_raw", w1_words, S)
+        xw = load_words("xw", x_words, T)
+        for r in range(PACK):
             load_scale_rows(nc.sync, ws_raw, 0, w1_scales, r)
-            load_scale_rows(nc.sync if r < 3 else nc.gpsimd, ws_raw, 4, w2_scales, r)
-        w2_raw = load_words("w2_raw", "w2_raw", w2_words, S)
+            load_scale_rows(nc.sync if r < PACK - 1 else nc.gpsimd, ws_raw, W2_ROWS, w2_scales, r)
+        w2_raw = load_words("w2_raw", w2_words, S)
         n1_t = load_list("n1_t", n1)
         cand_t = load_list("cand_t", cand)
         n2_t = load_list("n2_t", n2)
@@ -70,21 +79,13 @@ def tile_picked_twcputbgap_none_po_kernel(
         n3_t = load_list("n3_t", n3)
         n4_t = load_list("n4_t", n4)
 
-        def dealt(ap):
-            return ap.rearrange("p (t m) -> p m t", t=PACK)
-
-        def weave(copy, out, planes):
-            copy(out.rearrange("p (c i) t -> p c t i", i=4), planes.rearrange("p t (c i) -> p c t i", i=4))
-
-        def gather_scales(name, tag, lst):
-            tile = keep.tile([P, S], U8, name=name, tag=tag, align_bytes=64)
+        def gather_scales(name, lst):
+            tile = keep.tile([P, S], U8, name=name, align_bytes=64)
             nc.vector.tensor_copy(tile[:], xs[:].indirect(lst[:]))
             return tile
 
-        def gather_words(name, tag, lst, view):
-            tile = keep.tile([P, S], U32, name=name, tag=tag, align_bytes=64)
-            nc.vector.tensor_copy(view(tile[:]), xw[:].bitcast(U32).indirect(lst[:]))
-            return tile
+        def gather_words(out, lst):
+            nc.vector.tensor_copy(out, xw[:].bitcast(U32).indirect(lst[:]))
 
         def deal(name, dtype, src, line):
             tile = keep.tile([P, S], dtype, name=name, align_bytes=64)
@@ -94,129 +95,143 @@ def tile_picked_twcputbgap_none_po_kernel(
             )
             return tile
 
-        xo_s = gather_scales("xo_s", "xo_s", offs_t)
-        xo_w = gather_words("xo_w", "xo_w", offs_t, lambda ap: ap)
-        w1_d = deal("w1_d", I32, w1_raw, 4)
-        ws = deal("ws", U8, ws_raw, 16)
-        xt_s = gather_scales("xt_s", "xt_s", two_t)
-        xt_w = gather_words("xt_w", "reuse_a", two_t, lambda ap: ap)
-        w2_d = deal("w2_d", I32, w2_raw, 4)
-        xc_s_raw = gather_scales("xc_s_raw", "xc_s_raw", cand_t)
-        xc_w = gather_words("xc_w", "xc_w", cand_t, dealt)
-        xc_s = deal("xc_s", U8, xc_s_raw, 16)
+        xo_s = gather_scales("xo_s", offs_t)
+        xo_w = keep.tile([P, S], U32, name="xo_w", align_bytes=64)
+        gather_words(xo_w[:], offs_t)
+        w1_d = deal("w1_d", I32, w1_raw, WORDS_A_LINE)
+        ws = deal("ws", U8, ws_raw, BYTES_A_LINE)
+        xt_s = gather_scales("xt_s", two_t)
+        xt_w = keep.tile([P, S], U32, name="xt_w", tag="ws_raw_then_xt_w", align_bytes=64)
+        gather_words(xt_w[:], two_t)
+        w2_d = deal("w2_d", I32, w2_raw, WORDS_A_LINE)
+        xc_s_raw = gather_scales("xc_s_raw", cand_t)
+        xc_w = keep.tile([P, S], U32, name="xc_w", align_bytes=64)
+        gather_words(xc_w[:].rearrange("p (t m) -> p m t", t=PACK), cand_t)
+        xc_s = deal("xc_s", U8, xc_s_raw, BYTES_A_LINE)
 
-        def product(t, bank, lhs_w, lhs_s, first, rhs_w, rhs_s):
-            cols = slice(P * t, P * (t + 1))
-            acc = psum.tile([P, S], F32, name="acc", tag="bank%d" % bank)
+        def bank(index):
+            return psum.tile([P, S], F32, name="acc", tag="bank%d" % index)
+
+        def multiply(acc, t, lhs_w, lhs_s, first, rhs_w, rhs_s, cols):
+            rows = slice(P * t, P * (t + 1))
             nc.tensor.matmul_mx(
-                out=acc[:],
-                lhsT=lhs_w[:, cols].bitcast(FP8X4),
-                lhsT_scale=lhs_s[first:P, cols],
-                rhs=rhs_w[:].bitcast(FP8X4),
-                rhs_scale=rhs_s[:],
+                out=acc[:, cols],
+                lhsT=lhs_w[:, rows].bitcast(FP8X4),
+                lhsT_scale=lhs_s[first:P, rows],
+                rhs=rhs_w[:, cols].bitcast(FP8X4),
+                rhs_scale=rhs_s[:, cols],
                 start=True,
                 stop=True,
             )
-            return acc
 
-        y_acc = [product(t, t, w1_d, ws, 0, xo_w, xo_s) for t in range(PACK)]
-        d_acc = [product(t, PACK + t, w2_d, ws, 4, xt_w, xt_s) for t in range(PACK)]
+        def weave(copy, out, planes):
+            copy(out.rearrange("p (c i) t -> p c t i", i=WEAVE_RUN), planes.rearrange("p t (c i) -> p c t i", i=WEAVE_RUN))
+
+        def quantize(words, scales, woven):
+            nc.vector.quantize_mx(out=words.bitcast(FP8X4), scales=scales, in_=woven.rearrange("p j t -> p (j t)"))
+
+        every = slice(0, S)
+        halves = [slice(h * HALF, (h + 1) * HALF) for h in range(2)]
 
         z_planes = keep.tile([P, PACK, S], BF16, name="z_planes", align_bytes=64)
-        def round_plane(t, ds):
-            nc.vector.tensor_scalar(z_planes[:, t, :], ds[:], gs_t[:, t : t + 1], None, MULT)
+        ds = [keep.tile([P, S], F32, name="ds%d" % t) for t in range(PACK)]
+        d_sb = [keep.tile([P, S], F32, name="d_sb%d" % t) for t in range(PACK)]
+        y_term = [keep.tile([P, W], F32, name="y_term%d" % t) for t in range(PACK)]
+        d_pick = [keep.tile([P, W], F32, name="d_pick%d" % t) for t in range(PACK)]
 
-        ds_all = []
-        for t in range(PACK):
-            on_scalar = t == 2
-            ds = keep.tile([P, S], F32, name="ds%d" % t)
-            nc.scalar.activation(ds[:], y_acc[t][:], COPY)
-            d_sb = keep.tile([P, S], F32, name="d_sb%d" % t)
-            nc.scalar.activation(d_sb[:], d_acc[t][:], COPY, scale=2.0 if on_scalar else 1.0)
-            y_half = keep.tile([P, W], F32, name="y_half%d" % t)
-            d_pick = keep.tile([P, W], F32, name="d_pick%d" % t)
-            if on_scalar:
-                nc.scalar.activation(d_pick[:], d_sb[:].indirect(n2_t[:]), COPY)
-                nc.vector.tensor_tensor(y_half[:], ds[:].indirect(n1_t[:]), d_pick[:], SUB)
-                late = y_half
-            else:
-                nc.scalar.activation(y_half[:], ds[:].indirect(n1_t[:]), COPY, scale=-0.5)
-                nc.scalar.activation(d_pick[:], d_sb[:].indirect(n2_t[:]), COPY)
-                nc.vector.tensor_tensor(ds[:].indirect(n1_t[:]), d_pick[:], y_half[:], ADD)
-            ds_all.append(ds)
-            if t in (1, 2):
-                round_plane(t - 1, ds_all[t - 1])
-        nc.scalar.activation(ds_all[2][:].indirect(n1_t[:]), late[:], COPY, scale=-0.5)
-        round_plane(3, ds_all[3])
-        nc.scalar.activation(z_planes[:, 2, :], ds_all[2][:], COPY, scale=gs_t[:, 2:3])
+        def y_product(t, bank_index):
+            acc = bank(bank_index)
+            multiply(acc, t, w1_d, ws, 0, xo_w, xo_s, every)
+            nc.scalar.activation(ds[t][:], acc[:], COPY)
+
+        def d_product(t, bank_index, scale):
+            acc = bank(bank_index)
+            multiply(acc, t, w2_d, ws, W2_ROWS, xt_w, xt_s, every)
+            nc.scalar.activation(d_sb[t][:], acc[:], COPY, scale=scale)
+
+        def pick_y(t):
+            nc.scalar.activation(y_term[t][:], ds[t][:].indirect(n1_t[:]), COPY, scale=-0.5)
+
+        def pick_d(t):
+            nc.scalar.activation(d_pick[t][:], d_sb[t][:].indirect(n2_t[:]), COPY)
+
+        def put(t):
+            nc.vector.tensor_tensor(ds[t][:].indirect(n1_t[:]), d_pick[t][:], y_term[t][:], ADD)
+
+        def round_plane(t):
+            nc.vector.tensor_scalar(z_planes[:, t, :], ds[t][:], gs_t[:, t : t + 1], None, MULT)
+
+        for t in (0, 1):
+            y_product(t, t)
+        for t in (0, 1):
+            pick_y(t)
+        for t in (0, 1):
+            d_product(t, 2 + t, 1.0)
+        for t in (0, 1):
+            pick_d(t)
+            put(t)
+        y_product(2, 2)
+        d_product(2, 0, 2.0)
+        y_product(3, 3)
+        d_product(3, 1, 1.0)
+        for t in (0, 1):
+            round_plane(t)
+        pick_d(2)
+        nc.vector.tensor_tensor(y_term[2][:], ds[2][:].indirect(n1_t[:]), d_pick[2][:], SUB)
+        pick_y(3)
+        pick_d(3)
+        put(3)
+        nc.scalar.activation(ds[2][:].indirect(n1_t[:]), y_term[2][:], COPY, scale=-0.5)
+        round_plane(3)
+        nc.scalar.activation(z_planes[:, 2, :], ds[2][:], COPY, scale=gs_t[:, 2:3])
 
         z_w = keep.tile([P, S], U32, name="z_w", align_bytes=64)
         z_s = keep.tile([P, S], U8, name="z_s", align_bytes=64)
         z_in = keep.tile([P, S, PACK], BF16, name="z_in", align_bytes=64)
-        weave(nc.vector.tensor_copy, z_in[:, 0:256, :], z_planes[:, :, 0:256])
-        weave(nc.vector.tensor_copy, z_in[:, 256:384, :], z_planes[:, :, 256:384])
-        weave(nc.scalar.copy, z_in[:, 384:512, :], z_planes[:, :, 384:512])
-        s_acc = [psum.tile([P, S], F32, name="s_acc%d" % t, tag="bank%d" % t) for t in range(PACK)]
-        for h in range(2):
-            cols = slice(h * HALF, (h + 1) * HALF)
-            nc.vector.quantize_mx(out=z_w[:, cols].bitcast(FP8X4), scales=z_s[:, cols], in_=z_in[:, cols, :].rearrange("p j t -> p (j t)"))
+        weave(nc.vector.tensor_copy, z_in[:, 0:HALF, :], z_planes[:, :, 0:HALF])
+        weave(nc.vector.tensor_copy, z_in[:, HALF:Z_SPLIT, :], z_planes[:, :, HALF:Z_SPLIT])
+        weave(nc.scalar.copy, z_in[:, Z_SPLIT:S, :], z_planes[:, :, Z_SPLIT:S])
+        for cols in halves:
+            quantize(z_w[:, cols], z_s[:, cols], z_in[:, cols, :])
 
-        def score(t, cols):
-            rows = slice(P * t, P * (t + 1))
-            nc.tensor.matmul_mx(
-                out=s_acc[t][:, cols],
-                lhsT=xc_w[:, rows].bitcast(FP8X4),
-                lhsT_scale=xc_s[:, rows],
-                rhs=z_w[:, cols].bitcast(FP8X4),
-                rhs_scale=z_s[:, cols],
-                start=True,
-                stop=True,
-            )
+        neg_s = [keep.tile([P, S], F32, name="neg_s%d" % t) for t in range(PACK)]
+        first_accs = [bank(t) for t in (0, 1)]
+        for cols in halves:
+            for t in (0, 1):
+                multiply(first_accs[t], t, xc_w, xc_s, 0, z_w, z_s, cols)
+        nc.scalar.activation(neg_s[0][:], first_accs[0][:], COPY, scale=NEG_SIXTEENTH)
+        nc.vector.tensor_scalar(neg_s[1][:], first_accs[1][:], NEG_SIXTEENTH, None, MULT)
 
-        for h in range(2):
-            for t in range(2):
-                score(t, slice(h * HALF, (h + 1) * HALF))
-        for t in range(2, PACK):
-            score(t, slice(0, S))
-
-        neg_s = []
-        for t in range(PACK):
-            tile = keep.tile([P, S], F32, name="neg_s%d" % t)
-            if t % 2 == 0:
-                nc.scalar.activation(tile[:], s_acc[t][:], COPY, scale=-0.0625)
-            else:
-                nc.vector.tensor_scalar(tile[:], s_acc[t][:], -0.0625, None, MULT)
-            neg_s.append(tile)
+        def late_score(t):
+            acc = bank(t - 2)
+            multiply(acc, t, xc_w, xc_s, 0, z_w, z_s, every)
+            nc.scalar.activation(neg_s[t][:], acc[:], COPY, scale=NEG_SIXTEENTH)
 
         out_rows = out_0.rearrange("(p t) j -> p t j", t=PACK)
         o_w = keep.tile([P, S], I32, name="o_w", align_bytes=64)
         o_s = keep.tile([P, S], U8, name="o_s", align_bytes=64)
-        halves = []
+        o_half = [keep.tile([P, PACK, HALF], F32, name="o%d" % h) for h in range(2)]
+
+        def difference(t, h):
+            entries = slice(h * LIST_COLS, (h + 1) * LIST_COLS)
+            at_n3 = keep.tile([P, HALF], F32, name="at_n3_%d_%d" % (h, t))
+            nc.scalar.activation(at_n3[:], neg_s[t][:].indirect(n3_t[:, entries]), COPY)
+            nc.vector.tensor_tensor(o_half[h][:, t, :], neg_s[t][:].indirect(n4_t[:, entries]), at_n3[:], SUB)
+            if t % 2 == 1:
+                nc.sync.dma_start(out_rows[:, t - 1 : t + 1, halves[h]], o_half[h][:, t - 1 : t + 1, :])
+
         for h in range(2):
-            cols = slice(h * HALF, (h + 1) * HALF)
-            entries = slice(h * HALF // 16, (h + 1) * HALF // 16)
-            o = keep.tile([P, PACK, HALF], F32, name="o%d" % h)
             for t in range(PACK):
-                g = keep.tile([P, HALF], F32, name="g3_%d_%d" % (h, t))
-                nc.scalar.activation(g[:], neg_s[t][:].indirect(n3_t[:, entries]), COPY)
-                if t == PACK - 1:
-                    g4 = keep.tile([P, HALF], F32, name="g4_%d" % h)
-                    nc.scalar.activation(g4[:], neg_s[t][:].indirect(n4_t[:, entries]), COPY)
-                    nc.vector.tensor_tensor(o[:, t, :], g4[:], g[:], SUB)
-                else:
-                    nc.vector.tensor_tensor(o[:, t, :], neg_s[t][:].indirect(n4_t[:, entries]), g[:], SUB)
-                if t % 2 == 1:
-                    nc.sync.dma_start(out_rows[:, t - 1 : t + 1, cols], o[:, t - 1 : t + 1, :])
-            halves.append(o)
-        for h in range(2):
-            cols = slice(h * HALF, (h + 1) * HALF)
+                if h == 0 and t >= 2:
+                    late_score(t)
+                difference(t, h)
+
+        for h, copy in enumerate((nc.scalar.copy, nc.vector.tensor_copy)):
+            cols = halves[h]
             o_in = keep.tile([P, HALF, PACK], BF16, name="o_in%d" % h, align_bytes=64)
-            if h == 0:
-                weave(nc.scalar.copy, o_in[:], halves[h][:])
-            else:
-                weave(nc.vector.tensor_copy, o_in[:], halves[h][:])
-            nc.vector.quantize_mx(out=o_w[:, cols].bitcast(FP8X4), scales=o_s[:, cols], in_=o_in[:].rearrange("p j t -> p (j t)"))
+            weave(copy, o_in[:], o_half[h][:])
+            quantize(o_w[:, cols], o_s[:, cols], o_in[:])
             nc.sync.dma_start(as_words(out_1)[:, cols], o_w[:, cols])
-        for r in range(4):
+        for r in range(PACK):
             engine = nc.sync if r % 2 == 0 else nc.scalar
-            engine.dma_start(out_2[0][r:16:4, :].bitcast(I32), o_s[r:P:32, :].bitcast(I32))
+            engine.dma_start(out_2[0][r:SCALE_ROWS:PACK, :].bitcast(I32), o_s[r:P:QUADRANT, :].bitcast(I32))

from contextlib import ExitStack

import concourse.mybir as mybir

F32 = mybir.dt.float32
BF16 = mybir.dt.bfloat16
I32 = mybir.dt.int32
U32 = mybir.dt.uint32
U16 = mybir.dt.uint16
U8 = mybir.dt.uint8
FP8X4 = mybir.dt.float8_e4m3fn_x4
COPY = mybir.ActivationFunctionType.Copy
ADD = mybir.AluOpType.add
SUB = mybir.AluOpType.subtract
MULT = mybir.AluOpType.mult

P = 128
PACK = 4
QUADRANT = 32
SCALE_ROWS = 16
T = 2048
S = 512
W = 256
HALF = S // 2
LIST_COLS = HALF // 16
W2_ROWS = 4
WORDS_A_LINE = 4
BYTES_A_LINE = 16
WEAVE_RUN = 4
Z_SPLIT = 384
NEG_SIXTEENTH = -0.0625
FLOPS = 3 * 2 * 512 * 512 * 512


def tile_picked_twcputbgap_none_po_kernel(
    tc, x_words, x_scales, w1_words, w1_scales, w2_words, w2_scales, gs, offs, two, n1, n2, cand, n3, n4, out_0, out_1, out_2
):
    nc = tc.nc
    with ExitStack() as ctx:
        keep = ctx.enter_context(tc.tile_pool(name="keep", bufs=1))
        psum = ctx.enter_context(tc.psum_pool(name="psum", bufs=1))

        def as_words(dram):
            return dram[0].rearrange("p n t -> p (n t)").bitcast(I32)

        def load_list(name, dram):
            tile = keep.tile(list(dram.shape), U16, name=name)
            nc.sync.dma_start(tile[:], dram)
            return tile

        def load_words(name, dram, width):
            tile = keep.tile([P, width], I32, name=name, align_bytes=64)
            nc.sync.dma_start(tile[:], as_words(dram))
            return tile

        def load_scale_rows(engine, tile, first, dram, r):
            engine.dma_start(tile[first + r : P : QUADRANT, :].bitcast(I32), dram[0][r:SCALE_ROWS:PACK, :].bitcast(I32))

        xs = keep.tile([P, T], U8, name="xs", align_bytes=64)
        ws_raw = keep.tile([P, S], U8, name="ws_raw", tag="ws_raw_then_xt_w", align_bytes=64)
        nc.gpsimd.memset(ws_raw[:].bitcast(I32), 0)

        for q in range(P // QUADRANT):
            rows = x_scales[0][PACK * q : PACK * (q + 1), :].bitcast(I32).rearrange("r n -> (r n)")
            nc.sync.dma_start(xs[QUADRANT * q : QUADRANT * (q + 1), :].bitcast(I32), rows.partition_broadcast(QUADRANT // PACK))
        offs_t = load_list("offs_t", offs)
        two_t = load_list("two_t", two)
        w1_raw = load_words("w1_raw", w1_words, S)
        xw = load_words("xw", x_words, T)
        for r in range(PACK):
            load_scale_rows(nc.sync, ws_raw, 0, w1_scales, r)
            load_scale_rows(nc.sync if r < PACK - 1 else nc.gpsimd, ws_raw, W2_ROWS, w2_scales, r)
        w2_raw = load_words("w2_raw", w2_words, S)
        n1_t = load_list("n1_t", n1)
        cand_t = load_list("cand_t", cand)
        n2_t = load_list("n2_t", n2)
        gs_t = keep.tile([P, PACK], F32, name="gs_t")
        nc.sync.dma_start(gs_t[:], gs.rearrange("(p t) o -> p (t o)", t=PACK))
        n3_t = load_list("n3_t", n3)
        n4_t = load_list("n4_t", n4)

        def gather_scales(name, lst):
            tile = keep.tile([P, S], U8, name=name, align_bytes=64)
            nc.vector.tensor_copy(tile[:], xs[:].indirect(lst[:]))
            return tile

        def gather_words(out, lst):
            nc.vector.tensor_copy(out, xw[:].bitcast(U32).indirect(lst[:]))

        def deal(name, dtype, src, line):
            tile = keep.tile([P, S], dtype, name=name, align_bytes=64)
            nc.vector.tensor_copy(
                tile[:].rearrange("p (t c i) -> p c t i", t=PACK, i=line),
                src[:].rearrange("p (c i t) -> p c t i", t=PACK, i=line),
            )
            return tile

        xo_s = gather_scales("xo_s", offs_t)
        xo_w = keep.tile([P, S], U32, name="xo_w", align_bytes=64)
        gather_words(xo_w[:], offs_t)
        w1_d = deal("w1_d", I32, w1_raw, WORDS_A_LINE)
        ws = deal("ws", U8, ws_raw, BYTES_A_LINE)
        xt_s = gather_scales("xt_s", two_t)
        xt_w = keep.tile([P, S], U32, name="xt_w", tag="ws_raw_then_xt_w", align_bytes=64)
        gather_words(xt_w[:], two_t)
        w2_d = deal("w2_d", I32, w2_raw, WORDS_A_LINE)
        xc_s_raw = gather_scales("xc_s_raw", cand_t)
        xc_w = keep.tile([P, S], U32, name="xc_w", align_bytes=64)
        gather_words(xc_w[:].rearrange("p (t m) -> p m t", t=PACK), cand_t)
        xc_s = deal("xc_s", U8, xc_s_raw, BYTES_A_LINE)

        def bank(index):
            return psum.tile([P, S], F32, name="acc", tag="bank%d" % index)

        def multiply(acc, t, lhs_w, lhs_s, first, rhs_w, rhs_s, cols):
            rows = slice(P * t, P * (t + 1))
            nc.tensor.matmul_mx(
                out=acc[:, cols],
                lhsT=lhs_w[:, rows].bitcast(FP8X4),
                lhsT_scale=lhs_s[first:P, rows],
                rhs=rhs_w[:, cols].bitcast(FP8X4),
                rhs_scale=rhs_s[:, cols],
                start=True,
                stop=True,
            )

        def weave(copy, out, planes):
            copy(out.rearrange("p (c i) t -> p c t i", i=WEAVE_RUN), planes.rearrange("p t (c i) -> p c t i", i=WEAVE_RUN))

        def quantize(words, scales, woven):
            nc.vector.quantize_mx(out=words.bitcast(FP8X4), scales=scales, in_=woven.rearrange("p j t -> p (j t)"))

        every = slice(0, S)
        halves = [slice(h * HALF, (h + 1) * HALF) for h in range(2)]

        z_planes = keep.tile([P, PACK, S], BF16, name="z_planes", align_bytes=64)
        ds = [keep.tile([P, S], F32, name="ds%d" % t) for t in range(PACK)]
        d_sb = [keep.tile([P, S], F32, name="d_sb%d" % t) for t in range(PACK)]
        y_term = [keep.tile([P, W], F32, name="y_term%d" % t) for t in range(PACK)]
        d_pick = [keep.tile([P, W], F32, name="d_pick%d" % t) for t in range(PACK)]

        def y_product(t, bank_index):
            acc = bank(bank_index)
            multiply(acc, t, w1_d, ws, 0, xo_w, xo_s, every)
            nc.scalar.activation(ds[t][:], acc[:], COPY)

        def d_product(t, bank_index, scale):
            acc = bank(bank_index)
            multiply(acc, t, w2_d, ws, W2_ROWS, xt_w, xt_s, every)
            nc.scalar.activation(d_sb[t][:], acc[:], COPY, scale=scale)

        def pick_y(t):
            nc.scalar.activation(y_term[t][:], ds[t][:].indirect(n1_t[:]), COPY, scale=-0.5)

        def pick_d(t):
            nc.scalar.activation(d_pick[t][:], d_sb[t][:].indirect(n2_t[:]), COPY)

        def put(t):
            nc.vector.tensor_tensor(ds[t][:].indirect(n1_t[:]), d_pick[t][:], y_term[t][:], ADD)

        def round_plane(t):
            nc.vector.tensor_scalar(z_planes[:, t, :], ds[t][:], gs_t[:, t : t + 1], None, MULT)

        for t in (0, 1):
            y_product(t, t)
        for t in (0, 1):
            pick_y(t)
        for t in (0, 1):
            d_product(t, 2 + t, 1.0)
        for t in (0, 1):
            pick_d(t)
            put(t)
        y_product(2, 2)
        d_product(2, 0, 2.0)
        y_product(3, 3)
        d_product(3, 1, 1.0)
        for t in (0, 1):
            round_plane(t)
        pick_d(2)
        nc.vector.tensor_tensor(y_term[2][:], ds[2][:].indirect(n1_t[:]), d_pick[2][:], SUB)
        pick_y(3)
        pick_d(3)
        put(3)
        nc.scalar.activation(ds[2][:].indirect(n1_t[:]), y_term[2][:], COPY, scale=-0.5)
        round_plane(3)
        nc.scalar.activation(z_planes[:, 2, :], ds[2][:], COPY, scale=gs_t[:, 2:3])

        z_w = keep.tile([P, S], U32, name="z_w", align_bytes=64)
        z_s = keep.tile([P, S], U8, name="z_s", align_bytes=64)
        z_in = keep.tile([P, S, PACK], BF16, name="z_in", align_bytes=64)
        weave(nc.vector.tensor_copy, z_in[:, 0:HALF, :], z_planes[:, :, 0:HALF])
        weave(nc.vector.tensor_copy, z_in[:, HALF:Z_SPLIT, :], z_planes[:, :, HALF:Z_SPLIT])
        weave(nc.scalar.copy, z_in[:, Z_SPLIT:S, :], z_planes[:, :, Z_SPLIT:S])
        for cols in halves:
            quantize(z_w[:, cols], z_s[:, cols], z_in[:, cols, :])

        neg_s = [keep.tile([P, S], F32, name="neg_s%d" % t) for t in range(PACK)]
        first_accs = [bank(t) for t in (0, 1)]
        for cols in halves:
            for t in (0, 1):
                multiply(first_accs[t], t, xc_w, xc_s, 0, z_w, z_s, cols)
        nc.scalar.activation(neg_s[0][:], first_accs[0][:], COPY, scale=NEG_SIXTEENTH)
        nc.vector.tensor_scalar(neg_s[1][:], first_accs[1][:], NEG_SIXTEENTH, None, MULT)

        def late_score(t):
            acc = bank(t - 2)
            multiply(acc, t, xc_w, xc_s, 0, z_w, z_s, every)
            nc.scalar.activation(neg_s[t][:], acc[:], COPY, scale=NEG_SIXTEENTH)

        out_rows = out_0.rearrange("(p t) j -> p t j", t=PACK)
        o_w = keep.tile([P, S], I32, name="o_w", align_bytes=64)
        o_s = keep.tile([P, S], U8, name="o_s", align_bytes=64)
        o_half = [keep.tile([P, PACK, HALF], F32, name="o%d" % h) for h in range(2)]

        def difference(t, h):
            entries = slice(h * LIST_COLS, (h + 1) * LIST_COLS)
            at_n3 = keep.tile([P, HALF], F32, name="at_n3_%d_%d" % (h, t))
            nc.scalar.activation(at_n3[:], neg_s[t][:].indirect(n3_t[:, entries]), COPY)
            nc.vector.tensor_tensor(o_half[h][:, t, :], neg_s[t][:].indirect(n4_t[:, entries]), at_n3[:], SUB)
            if t % 2 == 1:
                nc.sync.dma_start(out_rows[:, t - 1 : t + 1, halves[h]], o_half[h][:, t - 1 : t + 1, :])

        for h in range(2):
            for t in range(PACK):
                if h == 0 and t >= 2:
                    late_score(t)
                difference(t, h)

        for h, copy in enumerate((nc.scalar.copy, nc.vector.tensor_copy)):
            cols = halves[h]
            o_in = keep.tile([P, HALF, PACK], BF16, name="o_in%d" % h, align_bytes=64)
            weave(copy, o_in[:], o_half[h][:])
            quantize(o_w[:, cols], o_s[:, cols], o_in[:])
            nc.sync.dma_start(as_words(out_1)[:, cols], o_w[:, cols])
        for r in range(PACK):
            engine = nc.sync if r % 2 == 0 else nc.scalar
            engine.dma_start(out_2[0][r:SCALE_ROWS:PACK, :].bitcast(I32), o_s[r:P:QUADRANT, :].bitcast(I32))
